import numpy as np
import ml_dtypes


def mxq(x, axis, fmt="e4m3"):
    dtype, down = {"e4m3": (ml_dtypes.float8_e4m3fn, 7), "e5m2": (ml_dtypes.float8_e5m2, 14)}[fmt]
    v = np.moveaxis(np.asarray(x, np.float32).astype(ml_dtypes.bfloat16).astype(np.float64), axis, -1)
    blocks = v.reshape(v.shape[:-1] + (-1, 32))
    amax = np.abs(blocks).max(-1, keepdims=True)
    byte = np.maximum(np.where(amax > 0, np.frexp(amax)[1] - 1 + 127, 0) - down, 1)
    scale = np.exp2(byte - 127.0)
    codes = (blocks / scale).astype(np.float32).astype(dtype).astype(np.float64)
    return np.moveaxis((codes * scale).reshape(v.shape), -1, axis)


WIDE = False


def mx_kscale(k):
    if not WIDE:
        return np.ones(k)
    levels = np.array([10, -10, 5, -5, 0])
    if k % 512:
        return np.exp2(np.random.permutation(np.resize(levels, k // 32))).repeat(32)
    a = np.empty((k // 512, 16))
    for p in range(k // 512):
        a[p, :8] = np.random.permutation(np.resize(levels, 8))
        for g in range(8):
            far = levels[np.abs(levels - a[p, g]) >= 10]
            a[p, g + 8] = far[np.random.randint(len(far))]
    return np.exp2(a.ravel()).repeat(32)


def f64(x):
    return np.asarray(x).astype(np.float64)


def striped(idx):
    return np.tile(idx.reshape(-1, 16).T, (8, 1)).astype(np.uint16)


def unstriped(offs):
    return offs[:16].T.reshape(-1).astype(np.int64)


E2M1 = np.array([0.0, 0.5, 1.0, 1.5, 2.0, 3.0, 4.0, 6.0, -0.0, -0.5, -1.0, -1.5, -2.0, -3.0, -4.0, -6.0])


def pack_weight(w, fmt):
    k, n = w.shape
    w = f64(np.asarray(w, np.float32).astype(ml_dtypes.bfloat16)).reshape(k // 32, 32, n)
    amax = np.abs(w).max(1)
    if fmt == "e4m3":
        byte = np.frexp(amax)[1] - 1 + 127 - 7
    else:
        mant, ex = np.frexp(amax / 6.0)
        byte = np.where(mant > 0.5, ex, ex - 1) + 127
    byte = np.clip(np.where(amax > 0, byte, 1), 1, 254)
    scaled = (w * np.exp2(127.0 - byte)[:, None, :]).reshape(k, n).astype(np.float32)
    by_word = np.ascontiguousarray(scaled.reshape(k // 512, 128, 4, n).transpose(0, 1, 3, 2))
    if fmt == "e4m3":
        words = by_word.astype(ml_dtypes.float8_e4m3fn).view(np.uint8)
    else:
        c = by_word.astype(ml_dtypes.float4_e2m1fn).view(np.uint8) & 0xF
        words = (c[..., 0::2] | (c[..., 1::2] << 4)).reshape(k // 512, 128, 2 * n)
    return np.ascontiguousarray(words), np.ascontiguousarray(byte.astype(np.uint8).reshape(k // 512, 16, n))


def unpack_weight(words, scales, fmt):
    g, _, n = scales.shape
    words = np.ascontiguousarray(words).reshape(g, 128, n, -1)
    if fmt == "e4m3":
        vals = words.view(ml_dtypes.float8_e4m3fn).astype(np.float64)
    else:
        nib = np.empty((g, 128, n, 4), np.uint8)
        nib[..., 0::2] = words & 0xF
        nib[..., 1::2] = words >> 4
        vals = E2M1[nib]
    vals = vals * np.repeat(np.exp2(scales.astype(np.float64) - 127.0), 8, axis=1)[..., None]
    return vals.transpose(0, 1, 3, 2).reshape(g * 512, n)


def gelu(v):
    return 0.5 * v * (1.0 + np.tanh(np.sqrt(2.0 / np.pi) * (v + 0.044715 * v**3)))


K, K1, T, S, H, T3, S2, P = 2048, 1024, 2048, 1024, 512, 4096, 1024, 512

def setup_inputs():
    n = np.random.standard_normal
    s = mx_kscale(K)[:, None]
    u = mx_kscale(H)[:, None]
    d = {}
    d["tab_words"], d["tab_scales"] = pack_weight(n((K, T)) * s, "e4m3")
    d["offs"] = striped(np.random.permutation(T)[:S])
    d["w1"] = (0.56 * n((K1, H)) / K ** 0.5 / s[:K1]).astype(np.float32)
    d["w4_words"], d["w4_scales"] = pack_weight(0.56 * n((K - K1, H)) / K ** 0.5 / s[K1:], "e2m1")
    d["gain"] = (np.exp(0.3 * n(H)) * u[:, 0]).astype(np.float32)
    d["tab2_words"], d["tab2_scales"] = pack_weight(n((H, T3)) / H ** 0.5 / u, "e4m3")
    d["offs2"] = striped(np.random.permutation(T3)[:S2])
    d["pos1"] = striped(np.random.permutation(S)[:P])
    d["pos2"] = striped(np.random.permutation(S)[:P])
    d["deed"] = (0.6 * n((S2, P))).astype(np.float32)
    return d

def reference(tab_words, tab_scales, offs, w1, w4_words, w4_scales, gain,
              tab2_words, tab2_scales, offs2, pos1, pos2, deed):
    v = unpack_weight(tab_words, tab_scales, "e4m3")[:, unstriped(offs)]
    v2 = unpack_weight(tab2_words, tab2_scales, "e4m3")[:, unstriped(offs2)]
    w4 = unpack_weight(w4_words, w4_scales, "e2m1")
    f = mxq(f64(w1), 0, "e4m3").T @ v[:K1] + w4.T @ v[K1:]
    h = (f + np.sin(f)) * f64(gain)[:, None]
    e = v2.T @ mxq(h, 0, "e4m3")
    orig = np.tanh(e[:, unstriped(pos1)])
    resurvey = np.tanh(e[:, unstriped(pos2)])
    return orig + resurvey - f64(deed)

@@ -1,0 +1,299 @@
+import math
+from contextlib import ExitStack
+
+import concourse.mybir as mybir
+from concourse.masks import make_identity
+
+K, K1, T, S, H, T3, S2, NP = 2048, 1024, 2048, 1024, 512, 4096, 1024, 512
+FLOPS = 2 * K * H * S + 2 * H * S2 * S
+
+F32 = mybir.dt.float32
+BF16 = mybir.dt.bfloat16
+I32 = mybir.dt.int32
+U32 = mybir.dt.uint32
+U16 = mybir.dt.uint16
+U8 = mybir.dt.uint8
+FP8X4 = mybir.dt.float8_e4m3fn_x4
+FP4X4 = mybir.dt.float4_e2m1fn_x4
+ACT = mybir.ActivationFunctionType
+ALU = mybir.AluOpType
+
+P = 128
+PACK = 4
+CHUNK = 128
+N_CHUNKS = S // CHUNK
+HALF = 512
+ROUNDER = 1.5 * 2.0**23
+
+
+def tile_list_boundary_marker_scores_kernel(
+    tc, tab_words, tab_scales, offs, w1, w4_words, w4_scales, gain,
+    tab2_words, tab2_scales, offs2, pos1, pos2, deed, out,
+):
+    nc = tc.nc
+    with ExitStack() as ctx:
+        keep = ctx.enter_context(tc.tile_pool(name="keep", bufs=1))
+        ring = ctx.enter_context(tc.tile_pool(name="ring", bufs=3))
+        psum = ctx.enter_context(tc.psum_pool(name="psum", bufs=8))
+
+        def held(name, shape, dtype):
+            return keep.tile(shape, dtype, name=name, align_bytes=64)
+
+        def entries(list_tile, first, count):
+            return list_tile[:, first // 16 : (first + count) // 16]
+
+        offs_sb = keep.tile([P, S // 16], U16, name="offs_sb")
+        offs2_sb = keep.tile([P, S2 // 16], U16, name="offs2_sb")
+        pos1_sb = keep.tile([P, NP // 16], U16, name="pos1_sb")
+        pos2_sb = keep.tile([P, NP // 16], U16, name="pos2_sb")
+
+        v_words = [held("v_words%d" % a, [P, T], I32) for a in range(4)]
+        v_rows = held("v_rows", [P, T], U8)
+        v_rows_picked = held("v_rows_picked", [P, S], U8)
+        v_planes = held("v_planes", [P, 4 * S], U8)
+        v_picked = [held("v_picked%d" % a, [P, S], I32) for a in range(4)]
+        w4_codes = held("w4_codes", [P, 2 * 2 * H], U8)
+        w4_plane = held("w4_plane", [P, 2 * H], U8)
+        w1_raw = [held("w1_raw%d" % a, [P, PACK, H], F32) for a in range(2)]
+        w1_bf = [held("w1_bf%d" % a, [P, PACK * H], BF16) for a in range(2)]
+        w1_codes = [held("w1_codes%d" % a, [P, H], U32) for a in range(2)]
+        w1_plane = [held("w1_plane%d" % a, [P, H], U8) for a in range(2)]
+        gain_sb = held("gain_sb", [P, 1, PACK], F32)
+        v2_words = held("v2_words", [P, T3], I32)
+        v2_rows = held("v2_rows", [P, T3], U8)
+        v2_rows_picked = held("v2_rows_picked", [P, S2], U8)
+        v2_picked = [held("v2_picked%d" % u, [P, HALF], I32) for u in range(2)]
+        v2_plane = held("v2_plane", [P, S2], U8)
+        deed_sb = [held("deed_sb%d" % u, [P, 4, NP], F32) for u in range(2)]
+        h_codes = [held("h_codes%d" % u, [P, HALF], U32) for u in range(2)]
+        h_plane = [held("h_plane%d" % u, [P, HALF], U8) for u in range(2)]
+        warm = held("warm", [P, 16], F32)
+        ident = held("ident", [P, P], F32)
+        make_identity(nc, ident[:])
+
+        nc.vector.memset(warm[:, 0:1], 0.0)
+        nc.vector.memset(w4_plane[:].bitcast(I32), 0)
+        nc.vector.memset(v_rows[64:128, :].bitcast(I32), 0)
+        nc.vector.memset(v_planes[:].bitcast(I32), 0)
+        nc.vector.memset(v2_rows[:].bitcast(I32), 0)
+        nc.vector.memset(v2_plane[:].bitcast(I32), 0)
+        nc.scalar.activation(warm[:, 8:9], warm[:, 0:1], ACT.Silu)
+
+        def load_v_words(a):
+            nc.sync.dma_start(v_words[a][:], tab_words[a].rearrange("p t i -> p (t i)").bitcast(I32))
+
+        def load_w1(a):
+            nc.sync.dma_start(w1_raw[a][:], w1[512 * a : 512 * (a + 1), :].rearrange("(p j) c -> p j c", j=PACK))
+
+        nc.sync.dma_start(offs_sb[:], offs)
+        nc.sync.dma_start(v_rows[0:64, :].bitcast(I32), tab_scales.bitcast(I32).rearrange("a q t -> q a t"))
+        load_v_words(2)
+        nc.sync.dma_start(
+            w4_codes[:].bitcast(I32).rearrange("p (a c) -> p a c", a=2),
+            w4_words.bitcast(I32).rearrange("a p c -> p a c"),
+        )
+        load_v_words(3)
+        for q in range(4):
+            nc.gpsimd.dma_start(
+                w4_plane[32 * q : 32 * q + 4, :].bitcast(I32).rearrange("r (a c) -> r a c", a=2),
+                w4_scales.bitcast(I32)[:, 4 * q : 4 * q + 4, :].rearrange("a r c -> r a c"),
+            )
+        load_v_words(0)
+        load_w1(0)
+        nc.sync.dma_start(offs2_sb[:], offs2)
+        nc.sync.dma_start(v2_rows[0:16, :].bitcast(I32), tab2_scales.bitcast(I32)[0])
+        load_w1(1)
+        load_v_words(1)
+        nc.vector.tensor_copy(v_rows_picked[:], v_rows[:].indirect(offs_sb[:]))
+        for q in range(4):
+            nc.scalar.dma_start(
+                v_planes[32 * q : 32 * q + 4, :].bitcast(I32),
+                v_rows_picked[16 * q : 16 * q + 16, :].bitcast(I32),
+            )
+        nc.sync.dma_start(gain_sb[:, 0, :], gain.rearrange("(p t) -> p t", t=PACK))
+        nc.sync.dma_start(v2_words[:], tab2_words[0].rearrange("p t i -> p (t i)").bitcast(I32))
+        nc.sync.dma_start(pos1_sb[:], pos1)
+        nc.sync.dma_start(pos2_sb[:], pos2)
+        for u in range(2):
+            nc.sync.dma_start(deed_sb[u][:], deed[HALF * u : HALF * (u + 1), :].rearrange("(i p) n -> p i n", p=P))
+
+        def pick_v(a, first, count):
+            nc.vector.tensor_copy(
+                v_picked[a][:, first : first + count].bitcast(U32),
+                v_words[a][:].bitcast(U32).indirect(entries(offs_sb, first, count)),
+            )
+
+        def quantise_w1(a):
+            nc.scalar.copy(
+                w1_bf[a][:].rearrange("p (c i j) -> p c j i", i=PACK, j=PACK),
+                w1_raw[a][:].rearrange("p j (c i) -> p c j i", i=PACK),
+            )
+            nc.vector.quantize_mx(out=w1_codes[a][:].bitcast(FP8X4), scales=w1_plane[a][:], in_=w1_bf[a][:])
+
+        f_bank = [psum.tile([P, PACK * CHUNK], F32, name="f_bank%d" % c, tag="bank") for c in range(N_CHUNKS)]
+
+        def first_product(a, c, start, stop):
+            if a < 2:
+                weight, plane = w1_codes[a][:].bitcast(FP8X4), w1_plane[a][:]
+            else:
+                weight = w4_codes[:, 2 * H * (a - 2) : 2 * H * (a - 1)].bitcast(FP4X4)
+                plane = w4_plane[:, H * (a - 2) : H * (a - 1)]
+            nc.tensor.matmul_mx(
+                out=f_bank[c][:],
+                lhsT=v_picked[a][:, CHUNK * c : CHUNK * (c + 1)].bitcast(FP8X4),
+                lhsT_scale=v_planes[:, S * a + CHUNK * c : S * a + CHUNK * (c + 1)],
+                rhs=weight,
+                rhs_scale=plane,
+                start=start,
+                stop=stop,
+            )
+
+        pick_v(2, 0, S)
+        for c in range(N_CHUNKS):
+            first_product(2, c, True, False)
+        pick_v(3, 0, S)
+        for c in range(N_CHUNKS):
+            first_product(3, c, False, False)
+        pick_v(0, 0, S)
+        nc.vector.tensor_copy(v2_rows_picked[:], v2_rows[:].indirect(offs2_sb[:]))
+        for q in range(4):
+            nc.gpsimd.dma_start(
+                v2_plane[32 * q : 32 * q + 4, :].bitcast(I32), v2_rows_picked[4 * q : 4 * q + 4, :].bitcast(I32)
+            )
+        quantise_w1(0)
+        for c in range(N_CHUNKS):
+            first_product(0, c, False, False)
+        quantise_w1(1)
+
+        f_sb, turns_up, turns, frac, sine, summed, h_bf = {}, {}, {}, {}, {}, {}, {}
+        kmode = ["V","V","V","V","V","V","V","V"]
+
+        def dealt(c):
+            return f_bank[c][:].rearrange("j (p t) -> j t p", t=PACK)
+
+        def by_slot(tile):
+            return tile[:].rearrange("j (t p) -> j t p", t=PACK)
+
+        def stage_copy(c):
+            f_sb[c] = ring.tile([P, H], F32, name="f_sb", bufs=5)
+            nc.scalar.copy(by_slot(f_sb[c]), dealt(c))
+            if kmode[c] == "S":
+                turns_up[c] = ring.tile([P, H], U32, name="turns_up")
+                nc.scalar.activation(by_slot(turns_up[c]), dealt(c), ACT.Copy, bias=ROUNDER, scale=1.0 / (2.0 * math.pi))
+
+        def stage_turns(c):
+            if kmode[c] == "S":
+                turns[c] = ring.tile([P, H], F32, name="turns")
+                nc.scalar.activation(turns[c][:], turns_up[c][:], ACT.Copy, bias=-ROUNDER, scale=1.0)
+            elif kmode[c] in ("V", "G"):
+                turns[c] = ring.tile([P, H], I32, name="turns")
+                eng = nc.vector if kmode[c] == "V" else nc.gpsimd
+                eng.tensor_scalar(turns[c][:], f_sb[c][:], 1.0 / (2.0 * math.pi), 0.0, ALU.mult, ALU.add)
+            else:
+                turns_up[c] = ring.tile([P, H], I32, name="turns_up")
+                eng = nc.vector if kmode[c] == "Vt" else nc.gpsimd
+                eng.tensor_scalar(turns_up[c][:], f_sb[c][:], 1.0 / (2.0 * math.pi), 10.0, ALU.mult, ALU.add)
+                turns[c] = ring.tile([P, H], F32, name="turns")
+                nc.vector.tensor_scalar(turns[c][:], turns_up[c][:], -10.0, None, ALU.add)
+
+        def stage_frac(c):
+            frac[c] = ring.tile([P, H], F32, name="frac")
+            nc.vector.scalar_tensor_tensor(
+                by_slot(frac[c]), dealt(c), 1.0 / (2.0 * math.pi), by_slot(turns[c]), ALU.mult, ALU.subtract
+            )
+
+        def turn(c, tile, first):
+            for t in range(PACK):
+                nc.tensor.matmul(
+                    summed[c][:, CHUNK * t : CHUNK * (t + 1)],
+                    tile[:, P * t : P * (t + 1)],
+                    ident[:],
+                    start=first and t == 0,
+                    stop=not first and t == PACK - 1,
+                    is_transpose=True,
+                )
+
+        def stage_sine(c):
+            sine[c] = ring.tile([P, H], F32, name="sine")
+            nc.scalar.activation(sine[c][:], frac[c][:], ACT.Sin, scale=2.0 * math.pi)
+            summed[c] = psum.tile([P, PACK * CHUNK], F32, name="summed", tag="bank")
+            turn(c, f_sb[c], True)
+
+        def stage_sum(c):
+            turn(c, sine[c], False)
+
+        def stage_gain(c):
+            h_bf[c] = ring.tile([P, PACK * CHUNK], BF16, name="h_bf", align_bytes=64)
+            nc.vector.tensor_tensor(
+                h_bf[c][:].rearrange("p (j t) -> p j t", t=PACK),
+                summed[c][:].rearrange("p (t j) -> p j t", t=PACK),
+                gain_sb[:].to_broadcast([P, CHUNK, PACK]),
+                ALU.mult,
+            )
+
+        def stage_quantise(c):
+            u, cols = c // 4, slice(CHUNK * (c % 4), CHUNK * (c % 4 + 1))
+            nc.vector.quantize_mx(out=h_codes[u][:, cols].bitcast(FP8X4), scales=h_plane[u][:, cols], in_=h_bf[c][:])
+
+        def stage_product(c):
+            if c % 2 == 0:
+                pick_v(1, CHUNK * c, 2 * CHUNK)
+            first_product(1, c, False, True)
+
+        def pick_v2(u):
+            nc.vector.tensor_copy(
+                v2_picked[u][:].bitcast(U32),
+                v2_words[:].bitcast(U32).indirect(entries(offs2_sb, HALF * u, HALF)),
+            )
+
+        scores, partial = {}, {}
+
+        def second_product(m, u):
+            if u == 0:
+                scores[m] = keep.tile([P, S], F32, name="scores%d" % m)
+            cols = slice(P * (m % 4), P * (m % 4 + 1))
+            e_bank = psum.tile([P, HALF], F32, name="e_bank", tag="bank")
+            nc.tensor.matmul_mx(
+                out=e_bank[:],
+                lhsT=v2_picked[m // 4][:, cols].bitcast(FP8X4),
+                lhsT_scale=v2_plane[:, P * m : P * (m + 1)],
+                rhs=h_codes[u][:].bitcast(FP8X4),
+                rhs_scale=h_plane[u][:],
+                start=True,
+                stop=True,
+            )
+            nc.scalar.activation(scores[m][:, HALF * u : HALF * (u + 1)], e_bank[:], ACT.Tanh)
+
+        def pick_first(m):
+            partial[m] = ring.tile([P, NP], F32, name="partial")
+            nc.vector.tensor_tensor(
+                partial[m][:], scores[m][:].indirect(pos1_sb[:]), deed_sb[m // 4][:, m % 4, :], ALU.subtract
+            )
+
+        def pick_second(m):
+            result = ring.tile([P, NP], F32, name="result")
+            nc.vector.tensor_tensor(result[:], scores[m][:].indirect(pos2_sb[:]), partial[m][:], ALU.add)
+            nc.sync.dma_start(out[P * m : P * (m + 1), :], result[:])
+
+        stages = [stage_product, stage_copy, stage_turns, stage_frac, stage_sine, stage_sum, stage_gain, stage_quantise]
+        for step in range(N_CHUNKS + len(stages) - 1):
+            for depth, stage in enumerate(stages):
+                c = step - depth
+                if 0 <= c < N_CHUNKS:
+                    stage(c)
+            if step == 4:
+                pick_v2(0)
+            if step - (len(stages) - 1) == 3:
+                for m in range(4):
+                    second_product(m, 0)
+        pick_v2(1)
+        for m in range(4):
+            second_product(m, 1)
+        for m in range(4, 8):
+            for u in range(2):
+                second_product(m, u)
+        for step in range(9):
+            if step < 8:
+                pick_first(step)
+            if step >= 1:
+                pick_second(step - 1)

@@ -60,10 +60,9 @@ def tile_list_boundary_marker_scores_kernel(
         w1_plane = [held("w1_plane%d" % a, [P, H], U8) for a in range(2)]
         gain_sb = held("gain_sb", [P, 1, PACK], F32)
         v2_words = held("v2_words", [P, T3], I32)
-        v2_rows = held("v2_rows", [P, T3], U8)
-        v2_rows_picked = held("v2_rows_picked", [P, S2], U8)
+        v2_plane = held("v2_plane", [P, T3], U8)
         v2_picked = [held("v2_picked%d" % u, [P, HALF], I32) for u in range(2)]
-        v2_plane = held("v2_plane", [P, S2], U8)
+        v2_plane_picked = held("v2_plane_picked", [P, S2], U8)
         deed_sb = [held("deed_sb%d" % u, [P, 4, NP], F32) for u in range(2)]
         h_codes = [held("h_codes%d" % u, [P, HALF], U32) for u in range(2)]
         h_plane = [held("h_plane%d" % u, [P, HALF], U8) for u in range(2)]
@@ -75,7 +74,6 @@ def tile_list_boundary_marker_scores_kernel(
         nc.vector.memset(w4_plane[:].bitcast(I32), 0)
         nc.vector.memset(v_rows[64:128, :].bitcast(I32), 0)
         nc.vector.memset(v_planes[:].bitcast(I32), 0)
-        nc.vector.memset(v2_rows[:].bitcast(I32), 0)
         nc.vector.memset(v2_plane[:].bitcast(I32), 0)
         nc.scalar.activation(warm[:, 8:9], warm[:, 0:1], ACT.Silu)
 
@@ -94,14 +92,18 @@ def tile_list_boundary_marker_scores_kernel(
         )
         load_v_words(3)
         for q in range(4):
-            nc.gpsimd.dma_start(
+            nc.scalar.dma_start(
                 w4_plane[32 * q : 32 * q + 4, :].bitcast(I32).rearrange("r (a c) -> r a c", a=2),
                 w4_scales.bitcast(I32)[:, 4 * q : 4 * q + 4, :].rearrange("a r c -> r a c"),
             )
         load_v_words(0)
         load_w1(0)
         nc.sync.dma_start(offs2_sb[:], offs2)
-        nc.sync.dma_start(v2_rows[0:16, :].bitcast(I32), tab2_scales.bitcast(I32)[0])
+        for q in range(4):
+            nc.sync.dma_start(
+                v2_plane[32 * q : 32 * q + 4, :].bitcast(I32),
+                tab2_scales.bitcast(I32)[0, 4 * q : 4 * q + 4, :],
+            )
         load_w1(1)
         load_v_words(1)
         nc.vector.tensor_copy(v_rows_picked[:], v_rows[:].indirect(offs_sb[:]))
@@ -155,11 +157,7 @@ def tile_list_boundary_marker_scores_kernel(
         for c in range(N_CHUNKS):
             first_product(3, c, False, False)
         pick_v(0, 0, S)
-        nc.vector.tensor_copy(v2_rows_picked[:], v2_rows[:].indirect(offs2_sb[:]))
-        for q in range(4):
-            nc.gpsimd.dma_start(
-                v2_plane[32 * q : 32 * q + 4, :].bitcast(I32), v2_rows_picked[4 * q : 4 * q + 4, :].bitcast(I32)
-            )
+        nc.vector.tensor_copy(v2_plane_picked[:], v2_plane[:].indirect(offs2_sb[:]))
         quantise_w1(0)
         for c in range(N_CHUNKS):
             first_product(0, c, False, False)
@@ -256,7 +254,7 @@ def tile_list_boundary_marker_scores_kernel(
             nc.tensor.matmul_mx(
                 out=e_bank[:],
                 lhsT=v2_picked[m // 4][:, cols].bitcast(FP8X4),
-                lhsT_scale=v2_plane[:, P * m : P * (m + 1)],
+                lhsT_scale=v2_plane_picked[:, P * m : P * (m + 1)],
                 rhs=h_codes[u][:].bitcast(FP8X4),
                 rhs_scale=h_plane[u][:],
                 start=True,

@@ -50,7 +50,7 @@ def tile_list_boundary_marker_scores_kernel(
         v_words = [held("v_words%d" % a, [P, T], I32) for a in range(4)]
         v_rows = held("v_rows", [P, T], U8)
         v_rows_picked = held("v_rows_picked", [P, S], U8)
-        v_planes = held("v_planes", [P, 4 * S], U8)
+        v_planes = held("v_planes", [P, 2 * S], U8)
         v_picked = [held("v_picked%d" % a, [P, S], I32) for a in range(4)]
         w4_codes = held("w4_codes", [P, 2 * 2 * H], U8)
         w4_plane = held("w4_plane", [P, 2 * H], U8)
@@ -84,7 +84,9 @@ def tile_list_boundary_marker_scores_kernel(
             nc.sync.dma_start(w1_raw[a][:], w1[512 * a : 512 * (a + 1), :].rearrange("(p j) c -> p j c", j=PACK))
 
         nc.sync.dma_start(offs_sb[:], offs)
-        nc.sync.dma_start(v_rows[0:64, :].bitcast(I32), tab_scales.bitcast(I32).rearrange("a q t -> q a t"))
+        scale_rows = tab_scales.bitcast(I32).rearrange("a (q r) t -> r (a q) t", r=4)
+        nc.sync.dma_start(v_rows[0:32, :].bitcast(I32), scale_rows[:, 8:16, :])
+        nc.scalar.dma_start(v_rows[32:64, :].bitcast(I32), scale_rows[:, 0:8, :])
         load_v_words(2)
         nc.sync.dma_start(
             w4_codes[:].bitcast(I32).rearrange("p (a c) -> p a c", a=2),
@@ -96,6 +98,12 @@ def tile_list_boundary_marker_scores_kernel(
                 w4_plane[32 * q : 32 * q + 4, :].bitcast(I32).rearrange("r (a c) -> r a c", a=2),
                 w4_scales.bitcast(I32)[:, 4 * q : 4 * q + 4, :].rearrange("a r c -> r a c"),
             )
+        nc.vector.tensor_copy(v_rows_picked[:], v_rows[:].indirect(offs_sb[:]))
+        for q in range(4):
+            nc.sync.dma_start(
+                v_planes[32 * q : 32 * q + 8, :].bitcast(I32),
+                v_rows_picked[q:64:4, :].bitcast(I32),
+            )
         load_v_words(0)
         load_w1(0)
         nc.sync.dma_start(offs2_sb[:], offs2)
@@ -106,12 +114,6 @@ def tile_list_boundary_marker_scores_kernel(
             )
         load_w1(1)
         load_v_words(1)
-        nc.vector.tensor_copy(v_rows_picked[:], v_rows[:].indirect(offs_sb[:]))
-        for q in range(4):
-            nc.scalar.dma_start(
-                v_planes[32 * q : 32 * q + 4, :].bitcast(I32),
-                v_rows_picked[16 * q : 16 * q + 16, :].bitcast(I32),
-            )
         nc.sync.dma_start(gain_sb[:, 0, :], gain.rearrange("(p t) -> p t", t=PACK))
         nc.sync.dma_start(v2_words[:], tab2_words[0].rearrange("p t i -> p (t i)").bitcast(I32))
         nc.sync.dma_start(pos1_sb[:], pos1)
@@ -143,7 +145,7 @@ def tile_list_boundary_marker_scores_kernel(
             nc.tensor.matmul_mx(
                 out=f_bank[c][:],
                 lhsT=v_picked[a][:, CHUNK * c : CHUNK * (c + 1)].bitcast(FP8X4),
-                lhsT_scale=v_planes[:, S * a + CHUNK * c : S * a + CHUNK * (c + 1)],
+                lhsT_scale=v_planes[(4 if a < 2 else 0) :, S * (a % 2) + CHUNK * c : S * (a % 2) + CHUNK * (c + 1)],
                 rhs=weight,
                 rhs_scale=plane,
                 start=start,
@@ -164,7 +166,7 @@ def tile_list_boundary_marker_scores_kernel(
         quantise_w1(1)
 
         f_sb, turns_up, turns, frac, sine, summed, h_bf = {}, {}, {}, {}, {}, {}, {}
-        kmode = ["V","V","V","V","V","V","V","V"]
+        kmode = ["G","G","G","G","G","G","G","G"]
 
         def dealt(c):
             return f_bank[c][:].rearrange("j (p t) -> j t p", t=PACK)
@@ -173,7 +175,7 @@ def tile_list_boundary_marker_scores_kernel(
             return tile[:].rearrange("j (t p) -> j t p", t=PACK)
 
         def stage_copy(c):
-            f_sb[c] = ring.tile([P, H], F32, name="f_sb", bufs=5)
+            f_sb[c] = ring.tile([P, H], F32, name="f_sb", bufs=8)
             nc.scalar.copy(by_slot(f_sb[c]), dealt(c))
             if kmode[c] == "S":
                 turns_up[c] = ring.tile([P, H], U32, name="turns_up")
@@ -195,7 +197,7 @@ def tile_list_boundary_marker_scores_kernel(
                 nc.vector.tensor_scalar(turns[c][:], turns_up[c][:], -10.0, None, ALU.add)
 
         def stage_frac(c):
-            frac[c] = ring.tile([P, H], F32, name="frac")
+            frac[c] = ring.tile([P, H], F32, name="frac", bufs=4)
             nc.vector.scalar_tensor_tensor(
                 by_slot(frac[c]), dealt(c), 1.0 / (2.0 * math.pi), by_slot(turns[c]), ALU.mult, ALU.subtract
             )
@@ -212,7 +214,7 @@ def tile_list_boundary_marker_scores_kernel(
                 )
 
         def stage_sine(c):
-            sine[c] = ring.tile([P, H], F32, name="sine")
+            sine[c] = ring.tile([P, H], F32, name="sine", bufs=4)
             nc.scalar.activation(sine[c][:], frac[c][:], ACT.Sin, scale=2.0 * math.pi)
             summed[c] = psum.tile([P, PACK * CHUNK], F32, name="summed", tag="bank")
             turn(c, f_sb[c], True)
@@ -273,15 +275,18 @@ def tile_list_boundary_marker_scores_kernel(
             nc.vector.tensor_tensor(result[:], scores[m][:].indirect(pos2_sb[:]), partial[m][:], ALU.add)
             nc.sync.dma_start(out[P * m : P * (m + 1), :], result[:])
 
-        stages = [stage_product, stage_copy, stage_turns, stage_frac, stage_sine, stage_sum, stage_gain, stage_quantise]
-        for step in range(N_CHUNKS + len(stages) - 1):
-            for depth, stage in enumerate(stages):
-                c = step - depth
-                if 0 <= c < N_CHUNKS:
-                    stage(c)
+        front = [stage_product, stage_copy, stage_turns, stage_frac, stage_sine, stage_sum]
+        for step in range(N_CHUNKS + len(front) - 1):
+            for depth, stage in enumerate(front):
+                if 0 <= step - depth < N_CHUNKS:
+                    stage(step - depth)
+        pick_v2(0)
+        for step in range(N_CHUNKS + 1):
+            if step < N_CHUNKS:
+                stage_gain(step)
+            if step >= 1:
+                stage_quantise(step - 1)
             if step == 4:
-                pick_v2(0)
-            if step - (len(stages) - 1) == 3:
                 for m in range(4):
                     second_product(m, 0)
         pick_v2(1)

@@ -4,7 +4,7 @@ from contextlib import ExitStack
 import concourse.mybir as mybir
 from concourse.masks import make_identity
 
-K, K1, T, S, H, T3, S2, NP = 2048, 1024, 2048, 1024, 512, 4096, 1024, 512
+K, T, S, H, T2, S2, PAIRS = 2048, 2048, 1024, 512, 4096, 1024, 512
 FLOPS = 2 * K * H * S + 2 * H * S2 * S
 
 F32 = mybir.dt.float32
@@ -20,10 +20,19 @@ ALU = mybir.AluOpType
 
 P = 128
 PACK = 4
+K_PASS = P * PACK
+PASSES = K // K_PASS
+W1_PASSES = 2
+QUADRANTS = 4
+ROWS = 4
+LIST_COLUMN = 16
 CHUNK = 128
 N_CHUNKS = S // CHUNK
 HALF = 512
-ROUNDER = 1.5 * 2.0**23
+PER_HALF = HALF // P
+M_TILES = S2 // P
+LAST_PIECE = 2 * CHUNK
+TURN = 2.0 * math.pi
 
 
 def tile_list_boundary_marker_scores_kernel(
@@ -40,51 +49,55 @@ def tile_list_boundary_marker_scores_kernel(
             return keep.tile(shape, dtype, name=name, align_bytes=64)
 
         def entries(list_tile, first, count):
-            return list_tile[:, first // 16 : (first + count) // 16]
+            return list_tile[:, first // LIST_COLUMN : (first + count) // LIST_COLUMN]
 
-        offs_sb = keep.tile([P, S // 16], U16, name="offs_sb")
-        offs2_sb = keep.tile([P, S2 // 16], U16, name="offs2_sb")
-        pos1_sb = keep.tile([P, NP // 16], U16, name="pos1_sb")
-        pos2_sb = keep.tile([P, NP // 16], U16, name="pos2_sb")
+        offs_sb = keep.tile([P, S // LIST_COLUMN], U16, name="offs_sb")
+        offs2_sb = keep.tile([P, S2 // LIST_COLUMN], U16, name="offs2_sb")
+        pos1_sb = keep.tile([P, PAIRS // LIST_COLUMN], U16, name="pos1_sb")
+        pos2_sb = keep.tile([P, PAIRS // LIST_COLUMN], U16, name="pos2_sb")
 
-        v_words = [held("v_words%d" % a, [P, T], I32) for a in range(4)]
+        v_words = [held("v_words%d" % a, [P, T], I32) for a in range(PASSES)]
         v_rows = held("v_rows", [P, T], U8)
         v_rows_picked = held("v_rows_picked", [P, S], U8)
         v_planes = held("v_planes", [P, 2 * S], U8)
-        v_picked = [held("v_picked%d" % a, [P, S], I32) for a in range(4)]
+        v_picked = [held("v_picked%d" % a, [P, S], I32) for a in range(PASSES)]
         w4_codes = held("w4_codes", [P, 2 * 2 * H], U8)
         w4_plane = held("w4_plane", [P, 2 * H], U8)
-        w1_raw = [held("w1_raw%d" % a, [P, PACK, H], F32) for a in range(2)]
-        w1_bf = [held("w1_bf%d" % a, [P, PACK * H], BF16) for a in range(2)]
-        w1_codes = [held("w1_codes%d" % a, [P, H], U32) for a in range(2)]
-        w1_plane = [held("w1_plane%d" % a, [P, H], U8) for a in range(2)]
+        w1_raw = [held("w1_raw%d" % a, [P, PACK, H], F32) for a in range(W1_PASSES)]
+        w1_bf = [held("w1_bf%d" % a, [P, PACK * H], BF16) for a in range(W1_PASSES)]
+        w1_codes = [held("w1_codes%d" % a, [P, H], U32) for a in range(W1_PASSES)]
+        w1_plane = [held("w1_plane%d" % a, [P, H], U8) for a in range(W1_PASSES)]
         gain_sb = held("gain_sb", [P, 1, PACK], F32)
-        v2_words = held("v2_words", [P, T3], I32)
-        v2_plane = held("v2_plane", [P, T3], U8)
+        v2_words = held("v2_words", [P, T2], I32)
+        v2_rows = held("v2_rows", [P, T2], U8)
+        v2_rows_picked = held("v2_rows_picked", [P, S2], U8)
         v2_picked = [held("v2_picked%d" % u, [P, HALF], I32) for u in range(2)]
-        v2_plane_picked = held("v2_plane_picked", [P, S2], U8)
-        deed_sb = [held("deed_sb%d" % u, [P, 4, NP], F32) for u in range(2)]
+        v2_plane = held("v2_plane", [P, S2], U8)
+        deed_sb = [held("deed_sb%d" % u, [P, PER_HALF, PAIRS], F32) for u in range(2)]
         h_codes = [held("h_codes%d" % u, [P, HALF], U32) for u in range(2)]
         h_plane = [held("h_plane%d" % u, [P, HALF], U8) for u in range(2)]
-        warm = held("warm", [P, 16], F32)
+        zero_in = held("zero_in", [P, 1], F32)
+        zero_bias = held("zero_bias", [P, 1], F32)
         ident = held("ident", [P, P], F32)
         make_identity(nc, ident[:])
 
-        nc.vector.memset(warm[:, 0:1], 0.0)
+        nc.vector.memset(zero_in[:], 0.0)
         nc.vector.memset(w4_plane[:].bitcast(I32), 0)
         nc.vector.memset(v_rows[64:128, :].bitcast(I32), 0)
         nc.vector.memset(v_planes[:].bitcast(I32), 0)
+        nc.vector.memset(v2_rows[:].bitcast(I32), 0)
         nc.vector.memset(v2_plane[:].bitcast(I32), 0)
-        nc.scalar.activation(warm[:, 8:9], warm[:, 0:1], ACT.Silu)
+        nc.scalar.activation(zero_bias[:], zero_in[:], ACT.Silu)
 
         def load_v_words(a):
             nc.sync.dma_start(v_words[a][:], tab_words[a].rearrange("p t i -> p (t i)").bitcast(I32))
 
         def load_w1(a):
-            nc.sync.dma_start(w1_raw[a][:], w1[512 * a : 512 * (a + 1), :].rearrange("(p j) c -> p j c", j=PACK))
+            rows = w1[K_PASS * a : K_PASS * (a + 1), :]
+            nc.sync.dma_start(w1_raw[a][:], rows.rearrange("(p i) c -> p i c", i=PACK))
 
         nc.sync.dma_start(offs_sb[:], offs)
-        scale_rows = tab_scales.bitcast(I32).rearrange("a (q r) t -> r (a q) t", r=4)
+        scale_rows = tab_scales.bitcast(I32).rearrange("a (q r) t -> r (a q) t", r=ROWS)
         nc.sync.dma_start(v_rows[0:32, :].bitcast(I32), scale_rows[:, 8:16, :])
         nc.scalar.dma_start(v_rows[32:64, :].bitcast(I32), scale_rows[:, 0:8, :])
         load_v_words(2)
@@ -93,33 +106,24 @@ def tile_list_boundary_marker_scores_kernel(
             w4_words.bitcast(I32).rearrange("a p c -> p a c"),
         )
         load_v_words(3)
-        for q in range(4):
-            nc.scalar.dma_start(
-                w4_plane[32 * q : 32 * q + 4, :].bitcast(I32).rearrange("r (a c) -> r a c", a=2),
-                w4_scales.bitcast(I32)[:, 4 * q : 4 * q + 4, :].rearrange("a r c -> r a c"),
+        for q in range(QUADRANTS):
+            nc.gpsimd.dma_start(
+                w4_plane[32 * q : 32 * q + ROWS, :].bitcast(I32).rearrange("r (a c) -> r a c", a=2),
+                w4_scales.bitcast(I32)[:, ROWS * q : ROWS * (q + 1), :].rearrange("a r c -> r a c"),
             )
         nc.vector.tensor_copy(v_rows_picked[:], v_rows[:].indirect(offs_sb[:]))
-        for q in range(4):
+        for q in range(QUADRANTS):
             nc.sync.dma_start(
-                v_planes[32 * q : 32 * q + 8, :].bitcast(I32),
-                v_rows_picked[q:64:4, :].bitcast(I32),
+                v_planes[32 * q : 32 * q + 2 * ROWS, :].bitcast(I32),
+                v_rows_picked[q:64:QUADRANTS, :].bitcast(I32),
             )
-        load_v_words(0)
-        load_w1(0)
         nc.sync.dma_start(offs2_sb[:], offs2)
-        for q in range(4):
-            nc.sync.dma_start(
-                v2_plane[32 * q : 32 * q + 4, :].bitcast(I32),
-                tab2_scales.bitcast(I32)[0, 4 * q : 4 * q + 4, :],
-            )
+        nc.sync.dma_start(v2_rows[0:16, :].bitcast(I32), tab2_scales.bitcast(I32)[0])
+        load_w1(0)
+        load_v_words(0)
         load_w1(1)
         load_v_words(1)
-        nc.sync.dma_start(gain_sb[:, 0, :], gain.rearrange("(p t) -> p t", t=PACK))
-        nc.sync.dma_start(v2_words[:], tab2_words[0].rearrange("p t i -> p (t i)").bitcast(I32))
-        nc.sync.dma_start(pos1_sb[:], pos1)
-        nc.sync.dma_start(pos2_sb[:], pos2)
-        for u in range(2):
-            nc.sync.dma_start(deed_sb[u][:], deed[HALF * u : HALF * (u + 1), :].rearrange("(i p) n -> p i n", p=P))
+        nc.sync.dma_start(gain_sb[:, 0, :], gain.rearrange("(p i) -> p i", i=PACK))
 
         def pick_v(a, first, count):
             nc.vector.tensor_copy(
@@ -129,25 +133,27 @@ def tile_list_boundary_marker_scores_kernel(
 
         def quantise_w1(a):
             nc.scalar.copy(
-                w1_bf[a][:].rearrange("p (c i j) -> p c j i", i=PACK, j=PACK),
-                w1_raw[a][:].rearrange("p j (c i) -> p c j i", i=PACK),
+                w1_bf[a][:].rearrange("p (c n i) -> p c i n", n=4, i=PACK),
+                w1_raw[a][:].rearrange("p i (c n) -> p c i n", n=4),
             )
             nc.vector.quantize_mx(out=w1_codes[a][:].bitcast(FP8X4), scales=w1_plane[a][:], in_=w1_bf[a][:])
 
-        f_bank = [psum.tile([P, PACK * CHUNK], F32, name="f_bank%d" % c, tag="bank") for c in range(N_CHUNKS)]
+        f_bank = [psum.tile([P, H], F32, name="f_bank%d" % c, tag="bank") for c in range(N_CHUNKS)]
 
         def first_product(a, c, start, stop):
-            if a < 2:
-                weight, plane = w1_codes[a][:].bitcast(FP8X4), w1_plane[a][:]
+            if a < W1_PASSES:
+                weight, weight_plane, first_row = w1_codes[a][:].bitcast(FP8X4), w1_plane[a][:], ROWS
             else:
-                weight = w4_codes[:, 2 * H * (a - 2) : 2 * H * (a - 1)].bitcast(FP4X4)
-                plane = w4_plane[:, H * (a - 2) : H * (a - 1)]
+                b = a - W1_PASSES
+                weight = w4_codes[:, 2 * H * b : 2 * H * (b + 1)].bitcast(FP4X4)
+                weight_plane, first_row = w4_plane[:, H * b : H * (b + 1)], 0
+            plane_column = S * (a % 2) + CHUNK * c
             nc.tensor.matmul_mx(
                 out=f_bank[c][:],
                 lhsT=v_picked[a][:, CHUNK * c : CHUNK * (c + 1)].bitcast(FP8X4),
-                lhsT_scale=v_planes[(4 if a < 2 else 0) :, S * (a % 2) + CHUNK * c : S * (a % 2) + CHUNK * (c + 1)],
+                lhsT_scale=v_planes[first_row:, plane_column : plane_column + CHUNK],
                 rhs=weight,
-                rhs_scale=plane,
+                rhs_scale=weight_plane,
                 start=start,
                 stop=stop,
             )
@@ -158,87 +164,82 @@ def tile_list_boundary_marker_scores_kernel(
         pick_v(3, 0, S)
         for c in range(N_CHUNKS):
             first_product(3, c, False, False)
-        pick_v(0, 0, S)
-        nc.vector.tensor_copy(v2_plane_picked[:], v2_plane[:].indirect(offs2_sb[:]))
+        nc.vector.tensor_copy(v2_rows_picked[:], v2_rows[:].indirect(offs2_sb[:]))
+        for q in range(QUADRANTS):
+            nc.gpsimd.dma_start(
+                v2_plane[32 * q : 32 * q + ROWS, :].bitcast(I32),
+                v2_rows_picked[ROWS * q : ROWS * (q + 1), :].bitcast(I32),
+            )
+        nc.sync.dma_start(v2_words[:], tab2_words[0].rearrange("p t i -> p (t i)").bitcast(I32))
+        nc.sync.dma_start(pos1_sb[:], pos1)
+        nc.sync.dma_start(pos2_sb[:], pos2)
+        for u in range(2):
+            nc.sync.dma_start(deed_sb[u][:], deed[HALF * u : HALF * (u + 1), :].rearrange("(m p) n -> p m n", p=P))
         quantise_w1(0)
+        pick_v(0, 0, S)
         for c in range(N_CHUNKS):
             first_product(0, c, False, False)
         quantise_w1(1)
 
-        f_sb, turns_up, turns, frac, sine, summed, h_bf = {}, {}, {}, {}, {}, {}, {}
-        kmode = ["G","G","G","G","G","G","G","G"]
+        f_sb, turns, frac, sine, summed, h_bf = {}, {}, {}, {}, {}, {}
 
-        def dealt(c):
-            return f_bank[c][:].rearrange("j (p t) -> j t p", t=PACK)
+        def f_by_run(c):
+            return f_bank[c][:].rearrange("j (p i) -> j i p", i=PACK)
 
-        def by_slot(tile):
-            return tile[:].rearrange("j (t p) -> j t p", t=PACK)
+        def by_run(tile):
+            return tile[:].rearrange("j (i p) -> j i p", i=PACK)
 
-        def stage_copy(c):
-            f_sb[c] = ring.tile([P, H], F32, name="f_sb", bufs=8)
-            nc.scalar.copy(by_slot(f_sb[c]), dealt(c))
-            if kmode[c] == "S":
-                turns_up[c] = ring.tile([P, H], U32, name="turns_up")
-                nc.scalar.activation(by_slot(turns_up[c]), dealt(c), ACT.Copy, bias=ROUNDER, scale=1.0 / (2.0 * math.pi))
+        def close_f(c):
+            if (CHUNK * c) % LAST_PIECE == 0:
+                pick_v(1, CHUNK * c, LAST_PIECE)
+            first_product(1, c, False, True)
 
-        def stage_turns(c):
-            if kmode[c] == "S":
-                turns[c] = ring.tile([P, H], F32, name="turns")
-                nc.scalar.activation(turns[c][:], turns_up[c][:], ACT.Copy, bias=-ROUNDER, scale=1.0)
-            elif kmode[c] in ("V", "G"):
-                turns[c] = ring.tile([P, H], I32, name="turns")
-                eng = nc.vector if kmode[c] == "V" else nc.gpsimd
-                eng.tensor_scalar(turns[c][:], f_sb[c][:], 1.0 / (2.0 * math.pi), 0.0, ALU.mult, ALU.add)
-            else:
-                turns_up[c] = ring.tile([P, H], I32, name="turns_up")
-                eng = nc.vector if kmode[c] == "Vt" else nc.gpsimd
-                eng.tensor_scalar(turns_up[c][:], f_sb[c][:], 1.0 / (2.0 * math.pi), 10.0, ALU.mult, ALU.add)
-                turns[c] = ring.tile([P, H], F32, name="turns")
-                nc.vector.tensor_scalar(turns[c][:], turns_up[c][:], -10.0, None, ALU.add)
+        def copy_f(c):
+            f_sb[c] = ring.tile([P, H], F32, name="f_sb", bufs=N_CHUNKS)
+            nc.scalar.copy(by_run(f_sb[c]), f_by_run(c))
 
-        def stage_frac(c):
+        def count_turns(c):
+            turns[c] = ring.tile([P, H], I32, name="turns")
+            nc.gpsimd.tensor_scalar(turns[c][:], f_sb[c][:], 1.0 / TURN, 0.0, ALU.mult, ALU.add)
+
+        def take_turns_off(c):
             frac[c] = ring.tile([P, H], F32, name="frac", bufs=4)
             nc.vector.scalar_tensor_tensor(
-                by_slot(frac[c]), dealt(c), 1.0 / (2.0 * math.pi), by_slot(turns[c]), ALU.mult, ALU.subtract
+                by_run(frac[c]), f_by_run(c), 1.0 / TURN, by_run(turns[c]), ALU.mult, ALU.subtract
             )
 
-        def turn(c, tile, first):
-            for t in range(PACK):
+        def transpose_into_sum(c, tile, opens):
+            for i in range(PACK):
                 nc.tensor.matmul(
-                    summed[c][:, CHUNK * t : CHUNK * (t + 1)],
-                    tile[:, P * t : P * (t + 1)],
+                    summed[c][:, CHUNK * i : CHUNK * (i + 1)],
+                    tile[:, P * i : P * (i + 1)],
                     ident[:],
-                    start=first and t == 0,
-                    stop=not first and t == PACK - 1,
+                    start=opens and i == 0,
+                    stop=not opens and i == PACK - 1,
                     is_transpose=True,
                 )
 
-        def stage_sine(c):
+        def take_sine(c):
             sine[c] = ring.tile([P, H], F32, name="sine", bufs=4)
-            nc.scalar.activation(sine[c][:], frac[c][:], ACT.Sin, scale=2.0 * math.pi)
+            nc.scalar.activation(sine[c][:], frac[c][:], ACT.Sin, bias=zero_bias[:], scale=TURN)
             summed[c] = psum.tile([P, PACK * CHUNK], F32, name="summed", tag="bank")
-            turn(c, f_sb[c], True)
+            transpose_into_sum(c, f_sb[c], True)
 
-        def stage_sum(c):
-            turn(c, sine[c], False)
+        def add_sine(c):
+            transpose_into_sum(c, sine[c], False)
 
-        def stage_gain(c):
+        def apply_gain(c):
             h_bf[c] = ring.tile([P, PACK * CHUNK], BF16, name="h_bf", align_bytes=64)
             nc.vector.tensor_tensor(
-                h_bf[c][:].rearrange("p (j t) -> p j t", t=PACK),
-                summed[c][:].rearrange("p (t j) -> p j t", t=PACK),
+                h_bf[c][:].rearrange("p (j i) -> p j i", i=PACK),
+                summed[c][:].rearrange("p (i j) -> p j i", i=PACK),
                 gain_sb[:].to_broadcast([P, CHUNK, PACK]),
                 ALU.mult,
             )
 
-        def stage_quantise(c):
-            u, cols = c // 4, slice(CHUNK * (c % 4), CHUNK * (c % 4 + 1))
+        def quantise_h(c):
+            u, cols = c // PER_HALF, slice(CHUNK * (c % PER_HALF), CHUNK * (c % PER_HALF + 1))
             nc.vector.quantize_mx(out=h_codes[u][:, cols].bitcast(FP8X4), scales=h_plane[u][:, cols], in_=h_bf[c][:])
-
-        def stage_product(c):
-            if c % 2 == 0:
-                pick_v(1, CHUNK * c, 2 * CHUNK)
-            first_product(1, c, False, True)
 
         def pick_v2(u):
             nc.vector.tensor_copy(
@@ -251,12 +252,12 @@ def tile_list_boundary_marker_scores_kernel(
         def second_product(m, u):
             if u == 0:
                 scores[m] = keep.tile([P, S], F32, name="scores%d" % m)
-            cols = slice(P * (m % 4), P * (m % 4 + 1))
+            cols = slice(P * (m % PER_HALF), P * (m % PER_HALF + 1))
             e_bank = psum.tile([P, HALF], F32, name="e_bank", tag="bank")
             nc.tensor.matmul_mx(
                 out=e_bank[:],
-                lhsT=v2_picked[m // 4][:, cols].bitcast(FP8X4),
-                lhsT_scale=v2_plane_picked[:, P * m : P * (m + 1)],
+                lhsT=v2_picked[m // PER_HALF][:, cols].bitcast(FP8X4),
+                lhsT_scale=v2_plane[:, P * m : P * (m + 1)],
                 rhs=h_codes[u][:].bitcast(FP8X4),
                 rhs_scale=h_plane[u][:],
                 start=True,
@@ -264,39 +265,47 @@ def tile_list_boundary_marker_scores_kernel(
             )
             nc.scalar.activation(scores[m][:, HALF * u : HALF * (u + 1)], e_bank[:], ACT.Tanh)
 
-        def pick_first(m):
-            partial[m] = ring.tile([P, NP], F32, name="partial")
+        def pick_original(m):
+            partial[m] = ring.tile([P, PAIRS], F32, name="partial")
             nc.vector.tensor_tensor(
-                partial[m][:], scores[m][:].indirect(pos1_sb[:]), deed_sb[m // 4][:, m % 4, :], ALU.subtract
+                partial[m][:],
+                scores[m][:].indirect(pos1_sb[:]),
+                deed_sb[m // PER_HALF][:, m % PER_HALF, :],
+                ALU.subtract,
             )
 
-        def pick_second(m):
-            result = ring.tile([P, NP], F32, name="result")
-            nc.vector.tensor_tensor(result[:], scores[m][:].indirect(pos2_sb[:]), partial[m][:], ALU.add)
-            nc.sync.dma_start(out[P * m : P * (m + 1), :], result[:])
+        def pick_resurvey(m):
+            result = ring.tile([P, PAIRS], F32, name="result")
+            width = PAIRS // 2 if m == M_TILES - 1 else PAIRS
+            for first in range(0, PAIRS, width):
+                cols = slice(first, first + width)
+                nc.vector.tensor_tensor(
+                    result[:, cols], scores[m][:].indirect(entries(pos2_sb, first, width)), partial[m][:, cols], ALU.add
+                )
+                nc.sync.dma_start(out[P * m : P * (m + 1), cols], result[:, cols])
 
-        front = [stage_product, stage_copy, stage_turns, stage_frac, stage_sine, stage_sum]
-        for step in range(N_CHUNKS + len(front) - 1):
-            for depth, stage in enumerate(front):
+        stages = [close_f, copy_f, count_turns, take_turns_off, take_sine, add_sine]
+        for step in range(N_CHUNKS + len(stages) - 1):
+            for depth, stage in enumerate(stages):
                 if 0 <= step - depth < N_CHUNKS:
                     stage(step - depth)
         pick_v2(0)
         for step in range(N_CHUNKS + 1):
             if step < N_CHUNKS:
-                stage_gain(step)
+                apply_gain(step)
             if step >= 1:
-                stage_quantise(step - 1)
-            if step == 4:
-                for m in range(4):
+                quantise_h(step - 1)
+            if step == PER_HALF:
+                for m in range(PER_HALF):
                     second_product(m, 0)
         pick_v2(1)
-        for m in range(4):
+        for m in range(PER_HALF):
             second_product(m, 1)
-        for m in range(4, 8):
+        for m in range(PER_HALF, M_TILES):
             for u in range(2):
                 second_product(m, u)
-        for step in range(9):
-            if step < 8:
-                pick_first(step)
+        for step in range(M_TILES + 1):
+            if step < M_TILES:
+                pick_original(step)
             if step >= 1:
-                pick_second(step - 1)
+                pick_resurvey(step - 1)

import math
from contextlib import ExitStack

import concourse.mybir as mybir
from concourse.masks import make_identity

K, T, S, H, T2, S2, PAIRS = 2048, 2048, 1024, 512, 4096, 1024, 512
FLOPS = 2 * K * H * S + 2 * H * S2 * S

F32 = mybir.dt.float32
BF16 = mybir.dt.bfloat16
I32 = mybir.dt.int32
U32 = mybir.dt.uint32
U16 = mybir.dt.uint16
U8 = mybir.dt.uint8
FP8X4 = mybir.dt.float8_e4m3fn_x4
FP4X4 = mybir.dt.float4_e2m1fn_x4
ACT = mybir.ActivationFunctionType
ALU = mybir.AluOpType

P = 128
PACK = 4
K_PASS = P * PACK
PASSES = K // K_PASS
W1_PASSES = 2
QUADRANTS = 4
ROWS = 4
LIST_COLUMN = 16
CHUNK = 128
N_CHUNKS = S // CHUNK
HALF = 512
PER_HALF = HALF // P
M_TILES = S2 // P
LAST_PIECE = 2 * CHUNK
TURN = 2.0 * math.pi


def tile_list_boundary_marker_scores_kernel(
    tc, tab_words, tab_scales, offs, w1, w4_words, w4_scales, gain,
    tab2_words, tab2_scales, offs2, pos1, pos2, deed, out,
):
    nc = tc.nc
    with ExitStack() as ctx:
        keep = ctx.enter_context(tc.tile_pool(name="keep", bufs=1))
        ring = ctx.enter_context(tc.tile_pool(name="ring", bufs=3))
        psum = ctx.enter_context(tc.psum_pool(name="psum", bufs=8))

        def held(name, shape, dtype):
            return keep.tile(shape, dtype, name=name, align_bytes=64)

        def entries(list_tile, first, count):
            return list_tile[:, first // LIST_COLUMN : (first + count) // LIST_COLUMN]

        offs_sb = keep.tile([P, S // LIST_COLUMN], U16, name="offs_sb")
        offs2_sb = keep.tile([P, S2 // LIST_COLUMN], U16, name="offs2_sb")
        pos1_sb = keep.tile([P, PAIRS // LIST_COLUMN], U16, name="pos1_sb")
        pos2_sb = keep.tile([P, PAIRS // LIST_COLUMN], U16, name="pos2_sb")

        v_words = [held("v_words%d" % a, [P, T], I32) for a in range(PASSES)]
        v_rows = held("v_rows", [P, T], U8)
        v_rows_picked = held("v_rows_picked", [P, S], U8)
        v_planes = held("v_planes", [P, 2 * S], U8)
        v_picked = [held("v_picked%d" % a, [P, S], I32) for a in range(PASSES)]
        w4_codes = held("w4_codes", [P, 2 * 2 * H], U8)
        w4_plane = held("w4_plane", [P, 2 * H], U8)
        w1_raw = [held("w1_raw%d" % a, [P, PACK, H], F32) for a in range(W1_PASSES)]
        w1_bf = [held("w1_bf%d" % a, [P, PACK * H], BF16) for a in range(W1_PASSES)]
        w1_codes = [held("w1_codes%d" % a, [P, H], U32) for a in range(W1_PASSES)]
        w1_plane = [held("w1_plane%d" % a, [P, H], U8) for a in range(W1_PASSES)]
        gain_sb = held("gain_sb", [P, 1, PACK], F32)
        v2_words = held("v2_words", [P, T2], I32)
        v2_rows = held("v2_rows", [P, T2], U8)
        v2_rows_picked = held("v2_rows_picked", [P, S2], U8)
        v2_picked = [held("v2_picked%d" % u, [P, HALF], I32) for u in range(2)]
        v2_plane = held("v2_plane", [P, S2], U8)
        deed_sb = [held("deed_sb%d" % u, [P, PER_HALF, PAIRS], F32) for u in range(2)]
        h_codes = [held("h_codes%d" % u, [P, HALF], U32) for u in range(2)]
        h_plane = [held("h_plane%d" % u, [P, HALF], U8) for u in range(2)]
        zero_in = held("zero_in", [P, 1], F32)
        zero_bias = held("zero_bias", [P, 1], F32)
        ident = held("ident", [P, P], F32)
        make_identity(nc, ident[:])

        nc.vector.memset(zero_in[:], 0.0)
        nc.vector.memset(w4_plane[:].bitcast(I32), 0)
        nc.vector.memset(v_rows[64:128, :].bitcast(I32), 0)
        nc.vector.memset(v_planes[:].bitcast(I32), 0)
        nc.vector.memset(v2_rows[:].bitcast(I32), 0)
        nc.vector.memset(v2_plane[:].bitcast(I32), 0)
        nc.scalar.activation(zero_bias[:], zero_in[:], ACT.Silu)

        def load_v_words(a):
            nc.sync.dma_start(v_words[a][:], tab_words[a].rearrange("p t i -> p (t i)").bitcast(I32))

        def load_w1(a):
            rows = w1[K_PASS * a : K_PASS * (a + 1), :]
            nc.sync.dma_start(w1_raw[a][:], rows.rearrange("(p i) c -> p i c", i=PACK))

        nc.sync.dma_start(offs_sb[:], offs)
        scale_rows = tab_scales.bitcast(I32).rearrange("a (q r) t -> r (a q) t", r=ROWS)
        nc.sync.dma_start(v_rows[0:32, :].bitcast(I32), scale_rows[:, 8:16, :])
        nc.scalar.dma_start(v_rows[32:64, :].bitcast(I32), scale_rows[:, 0:8, :])
        load_v_words(2)
        nc.sync.dma_start(
            w4_codes[:].bitcast(I32).rearrange("p (a c) -> p a c", a=2),
            w4_words.bitcast(I32).rearrange("a p c -> p a c"),
        )
        load_v_words(3)
        for q in range(QUADRANTS):
            nc.gpsimd.dma_start(
                w4_plane[32 * q : 32 * q + ROWS, :].bitcast(I32).rearrange("r (a c) -> r a c", a=2),
                w4_scales.bitcast(I32)[:, ROWS * q : ROWS * (q + 1), :].rearrange("a r c -> r a c"),
            )
        nc.vector.tensor_copy(v_rows_picked[:], v_rows[:].indirect(offs_sb[:]))
        for q in range(QUADRANTS):
            nc.sync.dma_start(
                v_planes[32 * q : 32 * q + 2 * ROWS, :].bitcast(I32),
                v_rows_picked[q:64:QUADRANTS, :].bitcast(I32),
            )
        nc.sync.dma_start(offs2_sb[:], offs2)
        nc.sync.dma_start(v2_rows[0:16, :].bitcast(I32), tab2_scales.bitcast(I32)[0])
        load_w1(0)
        load_v_words(0)
        load_w1(1)
        load_v_words(1)
        nc.sync.dma_start(gain_sb[:, 0, :], gain.rearrange("(p i) -> p i", i=PACK))

        def pick_v(a, first, count):
            nc.vector.tensor_copy(
                v_picked[a][:, first : first + count].bitcast(U32),
                v_words[a][:].bitcast(U32).indirect(entries(offs_sb, first, count)),
            )

        def quantise_w1(a):
            nc.scalar.copy(
                w1_bf[a][:].rearrange("p (c n i) -> p c i n", n=4, i=PACK),
                w1_raw[a][:].rearrange("p i (c n) -> p c i n", n=4),
            )
            nc.vector.quantize_mx(out=w1_codes[a][:].bitcast(FP8X4), scales=w1_plane[a][:], in_=w1_bf[a][:])

        f_bank = [psum.tile([P, H], F32, name="f_bank%d" % c, tag="bank") for c in range(N_CHUNKS)]

        def first_product(a, c, start, stop):
            if a < W1_PASSES:
                weight, weight_plane, first_row = w1_codes[a][:].bitcast(FP8X4), w1_plane[a][:], ROWS
            else:
                b = a - W1_PASSES
                weight = w4_codes[:, 2 * H * b : 2 * H * (b + 1)].bitcast(FP4X4)
                weight_plane, first_row = w4_plane[:, H * b : H * (b + 1)], 0
            plane_column = S * (a % 2) + CHUNK * c
            nc.tensor.matmul_mx(
                out=f_bank[c][:],
                lhsT=v_picked[a][:, CHUNK * c : CHUNK * (c + 1)].bitcast(FP8X4),
                lhsT_scale=v_planes[first_row:, plane_column : plane_column + CHUNK],
                rhs=weight,
                rhs_scale=weight_plane,
                start=start,
                stop=stop,
            )

        pick_v(2, 0, S)
        for c in range(N_CHUNKS):
            first_product(2, c, True, False)
        pick_v(3, 0, S)
        for c in range(N_CHUNKS):
            first_product(3, c, False, False)
        nc.vector.tensor_copy(v2_rows_picked[:], v2_rows[:].indirect(offs2_sb[:]))
        for q in range(QUADRANTS):
            nc.gpsimd.dma_start(
                v2_plane[32 * q : 32 * q + ROWS, :].bitcast(I32),
                v2_rows_picked[ROWS * q : ROWS * (q + 1), :].bitcast(I32),
            )
        nc.sync.dma_start(v2_words[:], tab2_words[0].rearrange("p t i -> p (t i)").bitcast(I32))
        nc.sync.dma_start(pos1_sb[:], pos1)
        nc.sync.dma_start(pos2_sb[:], pos2)
        for u in range(2):
            nc.sync.dma_start(deed_sb[u][:], deed[HALF * u : HALF * (u + 1), :].rearrange("(m p) n -> p m n", p=P))
        quantise_w1(0)
        pick_v(0, 0, S)
        for c in range(N_CHUNKS):
            first_product(0, c, False, False)
        quantise_w1(1)

        f_sb, turns, frac, sine, summed, h_bf = {}, {}, {}, {}, {}, {}

        def f_by_run(c):
            return f_bank[c][:].rearrange("j (p i) -> j i p", i=PACK)

        def by_run(tile):
            return tile[:].rearrange("j (i p) -> j i p", i=PACK)

        def close_f(c):
            if (CHUNK * c) % LAST_PIECE == 0:
                pick_v(1, CHUNK * c, LAST_PIECE)
            first_product(1, c, False, True)

        def copy_f(c):
            f_sb[c] = ring.tile([P, H], F32, name="f_sb", bufs=N_CHUNKS)
            nc.scalar.copy(by_run(f_sb[c]), f_by_run(c))

        def count_turns(c):
            turns[c] = ring.tile([P, H], I32, name="turns")
            nc.gpsimd.tensor_scalar(turns[c][:], f_sb[c][:], 1.0 / TURN, 0.0, ALU.mult, ALU.add)

        def take_turns_off(c):
            frac[c] = ring.tile([P, H], F32, name="frac", bufs=4)
            nc.vector.scalar_tensor_tensor(
                by_run(frac[c]), f_by_run(c), 1.0 / TURN, by_run(turns[c]), ALU.mult, ALU.subtract
            )

        def transpose_into_sum(c, tile, opens):
            for i in range(PACK):
                nc.tensor.matmul(
                    summed[c][:, CHUNK * i : CHUNK * (i + 1)],
                    tile[:, P * i : P * (i + 1)],
                    ident[:],
                    start=opens and i == 0,
                    stop=not opens and i == PACK - 1,
                    is_transpose=True,
                )

        def take_sine(c):
            sine[c] = ring.tile([P, H], F32, name="sine", bufs=4)
            nc.scalar.activation(sine[c][:], frac[c][:], ACT.Sin, bias=zero_bias[:], scale=TURN)
            summed[c] = psum.tile([P, PACK * CHUNK], F32, name="summed", tag="bank")
            transpose_into_sum(c, f_sb[c], True)

        def add_sine(c):
            transpose_into_sum(c, sine[c], False)

        def apply_gain(c):
            h_bf[c] = ring.tile([P, PACK * CHUNK], BF16, name="h_bf", align_bytes=64)
            nc.vector.tensor_tensor(
                h_bf[c][:].rearrange("p (j i) -> p j i", i=PACK),
                summed[c][:].rearrange("p (i j) -> p j i", i=PACK),
                gain_sb[:].to_broadcast([P, CHUNK, PACK]),
                ALU.mult,
            )

        def quantise_h(c):
            u, cols = c // PER_HALF, slice(CHUNK * (c % PER_HALF), CHUNK * (c % PER_HALF + 1))
            nc.vector.quantize_mx(out=h_codes[u][:, cols].bitcast(FP8X4), scales=h_plane[u][:, cols], in_=h_bf[c][:])

        def pick_v2(u):
            nc.vector.tensor_copy(
                v2_picked[u][:].bitcast(U32),
                v2_words[:].bitcast(U32).indirect(entries(offs2_sb, HALF * u, HALF)),
            )

        scores, partial = {}, {}

        def second_product(m, u):
            if u == 0:
                scores[m] = keep.tile([P, S], F32, name="scores%d" % m)
            cols = slice(P * (m % PER_HALF), P * (m % PER_HALF + 1))
            e_bank = psum.tile([P, HALF], F32, name="e_bank", tag="bank")
            nc.tensor.matmul_mx(
                out=e_bank[:],
                lhsT=v2_picked[m // PER_HALF][:, cols].bitcast(FP8X4),
                lhsT_scale=v2_plane[:, P * m : P * (m + 1)],
                rhs=h_codes[u][:].bitcast(FP8X4),
                rhs_scale=h_plane[u][:],
                start=True,
                stop=True,
            )
            nc.scalar.activation(scores[m][:, HALF * u : HALF * (u + 1)], e_bank[:], ACT.Tanh)

        def pick_original(m):
            partial[m] = ring.tile([P, PAIRS], F32, name="partial")
            nc.vector.tensor_tensor(
                partial[m][:],
                scores[m][:].indirect(pos1_sb[:]),
                deed_sb[m // PER_HALF][:, m % PER_HALF, :],
                ALU.subtract,
            )

        def pick_resurvey(m):
            result = ring.tile([P, PAIRS], F32, name="result")
            width = PAIRS // 2 if m == M_TILES - 1 else PAIRS
            for first in range(0, PAIRS, width):
                cols = slice(first, first + width)
                nc.vector.tensor_tensor(
                    result[:, cols], scores[m][:].indirect(entries(pos2_sb, first, width)), partial[m][:, cols], ALU.add
                )
                nc.sync.dma_start(out[P * m : P * (m + 1), cols], result[:, cols])

        stages = [close_f, copy_f, count_turns, take_turns_off, take_sine, add_sine]
        for step in range(N_CHUNKS + len(stages) - 1):
            for depth, stage in enumerate(stages):
                if 0 <= step - depth < N_CHUNKS:
                    stage(step - depth)
        pick_v2(0)
        for step in range(N_CHUNKS + 1):
            if step < N_CHUNKS:
                apply_gain(step)
            if step >= 1:
                quantise_h(step - 1)
            if step == PER_HALF:
                for m in range(PER_HALF):
                    second_product(m, 0)
        pick_v2(1)
        for m in range(PER_HALF):
            second_product(m, 1)
        for m in range(PER_HALF, M_TILES):
            for u in range(2):
                second_product(m, u)
        for step in range(M_TILES + 1):
            if step < M_TILES:
                pick_original(step)
            if step >= 1:
                pick_resurvey(step - 1)
